import numpy as np, ml_dtypes
CORES = [24,25,26,27,28,29,30,31]
N = 8
BF = ml_dtypes.bfloat16
def gentries(a):
    return np.ascontiguousarray(a.reshape(8, 16, -1).transpose(0, 2, 1)).reshape(8, -1)
def gtable(e):
    e = np.asarray(e); return np.ascontiguousarray(e.reshape(8, -1, 16).transpose(0, 2, 1)).reshape(128, -1).astype(np.int32)
def f(rng, *shape):
    return (rng.standard_normal(shape, dtype=np.float32) * np.exp2(rng.integers(-2, 3, shape[:-1] + (1,)))).astype(BF)
def wide(rng, *shape):
    v = f(rng, *shape).astype(np.float32); k = shape[:-2] + (1, shape[-1])
    return (v * np.exp2(rng.integers(-6, 7, k)) * (rng.random(k) > 0.0625)).astype(BF)
M, A, L, C, SR, SA = 2048, 1024, 2, 6, 256, 128
def first(l):
    return M + N * SR + (l - 1) * (A + N * SA)
def glists(e):
    return np.stack([gtable(e[r].reshape(8, -1)) for r in range(N)])
def grow(rng, n):
    v = rng.standard_exponential((N, 8, 16, n), dtype=np.float32) * (rng.random((N, 8, 16, n)) < 0.75) * (0.5 + rng.random((N, 8, 1, n)))
    return np.add.accumulate(v, axis=2).reshape(N, 128, n).astype(BF)
def draw_parts(rng):
    e = np.zeros((N, 8, L, 2 * C, A), np.int64); k = (N, 8, 2 * C, A)
    for l in range(1, L + 1):
        e[:, :, l - 1] = rng.integers(0, first(l), k)
        if l > 1: e[:, :, l - 1] = np.where(rng.random(k) < 0.5, rng.integers(first(l - 1), first(l), k), e[:, :, l - 1])
    return e
def draw(rng, e):
    return {"sup": grow(rng, M), "cap": grow(rng, L * A), "stock": (8 * rng.random((N, 128, L * A)) * (rng.random((N, 128, L * A)) < 0.8)).astype(BF), "parts": glists(e),
            "ship": glists(rng.integers(0, M, (N, 8, N * SR))), "hand": glists(rng.integers(0, A, (N, 8, (L - 1) * N * SA)))}
def setup_inputs(rng):
    return draw(rng, draw_parts(rng))
def setup_inputs_ties(rng):
    e = draw_parts(rng); e[:, :, :, 1:C] = np.where(rng.random((N, 8, L, C - 1, A)) < 0.3, e[:, :, :, :1], e[:, :, :, 1:C])
    e[:, :, :, C:] = np.where(rng.random((N, 8, L, C, A)) < 0.2, e[:, :, :, :C], e[:, :, :, C:])
    d = draw(rng, e)
    d["sup"] = np.add.accumulate(rng.integers(0, 2, (N, 8, 16, M)), axis=2).reshape(N, 128, M).astype(np.float32).astype(BF)
    d["cap"] = np.add.accumulate(rng.integers(0, 3, (N, 8, 16, L * A)), axis=2).reshape(N, 128, L * A).astype(np.float32).astype(BF)
    d["stock"] = rng.integers(0, 4, (N, 128, L * A)).astype(np.float32).astype(BF); return d
def setup_inputs_ends(rng):
    e = draw_parts(rng)
    for l in range(1, L + 1):
        b = [0, M - 1, M, M + N * SR - 1]
        for m in range(1, l): b += [first(m), first(m) + A - 1, first(m) + A, first(m + 1) - 1]
        k = (N, 8, 2 * C, A); e[:, :, l - 1] = np.where(rng.random(k) < 0.5, rng.choice(np.array(b), k), e[:, :, l - 1])
        for r in range(N):
            q = (r + 1) % N
            for g in range(8):
                if l == 1: e[r, g, 0, 0, :SR] = M + q * SR + rng.permutation(SR)
                else: e[r, g, l - 1, 0, :SA] = first(l - 1) + A + q * SA + rng.permutation(SA)
    d = draw(rng, e)
    s = rng.integers(0, M, (N, 8, N, SR)); s[..., 0] = 0; s[..., -1] = M - 1; d["ship"] = glists(s)
    h = rng.integers(0, A, (N, 8, L - 1, N, SA)); h[..., 0] = A - 1; h[..., -1] = 0; d["hand"] = glists(h); return d
def setup_inputs_one(rng):
    e = np.zeros((N, 8, L, 2 * C, A), np.int64); a = rng.integers(1, N); k = (8, 2 * C, A)
    for r in range(N):
        q = (r + a) % N; e[r, :, 0] = M + q * SR + rng.integers(0, SR, k)
        for l in range(2, L + 1): e[r, :, l - 1] = first(l - 1) + A + q * SA + rng.integers(0, SA, k)
    d = draw(rng, e); s = rng.integers(0, M, (N, 8, N, SR)); q = rng.integers(0, N); s[q] = s[q][..., :1]; d["ship"] = glists(s); return d
def setup_inputs_late(rng):
    d = setup_inputs(rng); v = d["sup"].astype(np.float32).reshape(N, 8, 16, M); v[:, :, 15] = 64 - v[:, :, 14]; d["sup"] = v.reshape(N, 128, M).astype(BF)
    c = d["cap"].astype(np.float32).reshape(N, 8, 16, L * A); t = rng.integers(0, 14, (N, 8, 1, L * A))
    d["cap"] = np.where(np.arange(16)[:, None] < t - 4, np.float32(0), 8 * c).reshape(N, 128, L * A).astype(BF); return d
def setup_inputs_spread(rng):
    d = setup_inputs(rng)
    for k, n in (("sup", M), ("cap", L * A), ("stock", L * A)): d[k] = (wide(rng, N, 128, n).astype(np.float32) * np.float32(2.0 ** 40)).astype(BF)
    return d
def check_inputs(d):
    bad = []
    try:
        for k in ("sup", "cap", "stock"):
            v = d[k].astype(np.float32)
            if not (np.isfinite(v).all() and (np.abs(v) <= 2.0 ** 60).all()): bad.append(k)
        e = np.stack([gentries(v) for v in d["parts"]]).reshape(N, 8, L, 2 * C * A)
        if any((e[:, :, l - 1] < 0).any() or (e[:, :, l - 1] >= first(l)).any() for l in range(1, L + 1)): bad.append("parts")
        for k, n in (("ship", M), ("hand", A)):
            if (d[k] < 0).any() or (d[k] >= n).any(): bad.append(k)
    except Exception:
        bad.append("shapes")
    return bad
def reference(sup, cap, stock, parts, ship, hand):
    raw = sup.astype(np.float32).reshape(N, 8, 16, M); ca = cap.astype(np.float32).reshape(N, 8, 16, L, A); st = stock.astype(np.float32).reshape(N, 8, 16, L, A)
    e = [gentries(v).reshape(8, L, 1, 2 * C * A) for v in parts]; sh = [gentries(v).reshape(8, 1, N, SR) for v in ship]; ha = [gentries(v).reshape(8, 1, L - 1, N, SA) for v in hand]
    w = np.zeros((N, 8, 16, first(L)), np.float32); now = np.zeros((N, 8, 16, A), np.float32)
    w[..., :M] = raw; h = A // 2
    for r in range(N):
        for q in range(N): w[r, :, :, M + q * SR:M + (q + 1) * SR] = np.take_along_axis(raw[q], sh[q][:, :, r], 2)
    for l in range(1, L + 1):
        for r in range(N):
            v = np.take_along_axis(w[r], e[r][:, l - 1], 2).reshape(8, 16, 2 * C, A)
            i = np.argmin(v[:, 15, :C], axis=1)
            hit = np.arange(C)[:, None] == i[:, None]
            z = np.min(np.where(hit[:, None], v[:, :, C:], v[:, :, :C]), axis=2)
            s = np.zeros_like(z); s[:, 1:, :h] = z[:, :-1, :h]; s[:, 2:, h:] = z[:, :-2, h:]
            now[r] = np.minimum(s, ca[r, :, :, l - 1]) + st[r, :, :, l - 1]
        if l < L:
            b = first(l); w[:, :, :, b:b + A] = now
            for r in range(N):
                for q in range(N): w[r, :, :, b + A + q * SA:b + A + (q + 1) * SA] = np.take_along_axis(now[q], ha[q][:, :, l - 1, r], 2)
    return {"y": now.reshape(N, 128, A)}

from concourse.bass import DstId, RemoteDMATransfer
from concourse.mybir import AluOpType as Op, ActivationFunctionType as Act

M, A, C, SR, SA, N = 2048, 1024, 6, 256, 128, 8
BIG = float(2 ** 80)
CH = [[(0, 256, 48), (256, 512, 40), (512, 768, 24), (768, 1024, 8)],
      [(0, 256, 48), (256, 512, 40), (512, 768, 24), (768, 1024, 8)]]
PC = [[(0, 256, "F"), (256, 512, "S"), (512, 768, "F"), (768, 1024, "S")],
      [(0, 256, "F"), (256, 512, "S"), (512, 768, "F"), (768, 896, "S"), (896, 1024, "S")]]
PIECE = 24
SMAX = 7 * 640
ORDER = """l_sup l_ship i_p one l_p0 z6 l_c0 i_n i_j t1 l_k0 z7 d1 d2 tc r6 req rlt rge j1 S1 su j2 St gsv gsa send1 arr1 own1 wp1
j3 S2 bc neg B Sh0 Sh1 Mk0 Mk1 A0 A1 o1_0_0 o1_0_1 o1_0_2 o1_0_3 o1_0_4 o1_0_5 Sf0 Sf1 r7 dl0 cp0_1 cp0_3 mc0 z8
g1a0_0 g1a0_1 g1v0_0_72 l_hand l_p1 l_c1 g1a0_2 g1v0_0_48 l_k1 g1v0_1_80 ext0_0 g1v0_1_56 ext0_1 g1v0_3_88 scn0_0 low0_0 eq0_0
hit0_0 g1v0_2_72 g1a0_3 mul0_0 scn0_1 add0_0 ext0_2 wp2 low0_1 cnv0_0 eq0_1 hit0_1 g20_0_0 ext0_3 scn0_2 g20_0_1 mul0_1 cast
low0_2 g20_0_2 eq0_2 add0_1 g20_0_3 cnv0_1 g20_1_4 g20_1_0 hit0_2 scn0_3 low0_3 mul0_2 eq0_3 g20_0_4 g20_1_2 add0_2 hit0_3
mul0_3 cnv0_2 g20_1_1 add0_3 g20_2_0 prq0_1 cnv0_3 g20_1_5 g20_1_3 g20_3_3 g20_3_5 g20_2_1 g20_0_5 g20_2_2 prq0_0 g20_3_0
g20_3_1 g20_3_4 fnq0_0 red0_1 g20_3_2 fin0_0 fnq0_1 evq0_0 prq0_2 g20_2_3 evq0_1 g20_2_4 fin0_1 g20_2_5 fnq0_2 red0_3 hu
prq0_3 fnq0_3 evq0_3 fin0_3 evq0_2 hav haa send2 arr2 fin0_2 evp0 evp1 hbv hba send3 own2 own3 cp1_1
o1_1_0 o1_1_1 o1_1_2 o1_1_3 o1_1_4 o1_1_5 dl1 mc1
g1a1_0 g1v1_0_72 g1v1_0_48 ext1_0 g1a1_1 g1v1_1_80 g1a1_2 g1v1_1_56 scn1_0 ext1_1 g1a1_3 g1v1_3_88 low1_0 eq1_0 g1v1_2_72
hit1_0 mul1_0 scn1_1 add1_0 ext1_2 low1_1 cnv1_0 eq1_1 hit1_1 arr3 g21_0_0 scn1_2 g21_0_1 mul1_1 low1_2 g21_0_2 eq1_2 add1_1
g21_0_3 ext1_3 cp1_3 scn1_3 cnv1_1 g21_1_0 g21_1_1 g21_1_4 g21_1_5 low1_3 g21_1_3 hit1_2 mul1_2 g21_1_2 eq1_3 cp1_4 add1_2
g21_0_4 cnv1_2 hit1_3 mul1_3 pre1_0 g21_2_0 add1_3 g21_2_1 cnv1_3 g21_3_2 g21_3_3 pre1_2 g21_3_1 g21_3_5 g21_2_2 g21_4_3
g21_4_1 g21_0_5 g21_3_0 fin1_0 pre1_3 g21_2_3 g21_4_4 g21_3_4 g21_4_0 red1_1 pre1_1 fin1_1 g21_4_5 g21_2_4 red1_3 fin1_3
ev1_0 st1_0 g21_2_5 g21_4_2 pre1_4 ev1_1 st1_1 ev1_3 fin1_2 st1_3 red1_4 ev1_2 st1_2 fin1_4 ev1_4 st1_4""".split()
SCRATCH = {
    "W1": ("sbuf", [128, 4096], "bfloat16"), "W2": ("sbuf", [128, 6144], "float32"), "WP": ("sbuf", [128, 6144], "bfloat16"),
    "SH": ("sbuf", [128, 2048], "bfloat16"), "HA": ("sbuf", [128, 1024], "bfloat16"), "HB": ("sbuf", [128, 1024], "float32"),
    "ship32": ("sbuf", [128, 128], "int32"), "shipu": ("sbuf", [128, 128], "uint16"),
    "hand32": ("sbuf", [128, 64], "int32"), "handu": ("sbuf", [128, 64], "uint16"),
    "p32": ("sbuf", [128, 2, 12, 64], "int32"), "delta": ("sbuf", [128, 2, 6, 64], "float32"),
    "off1": ("sbuf", [128, 768], "uint16"), "off2": ("sbuf", [128, 768], "uint16"),
    "V0": ("sbuf", [128, 6144], "bfloat16"), "V1": ("sbuf", [128, 6144], "bfloat16"),
    "Mn": ("sbuf", [128, 768], "float32"), "M5": ("sbuf", [128, 128], "float32"), "eq": ("sbuf", [128, 768], "bfloat16"),
    "cs": ("sbuf", [128, 2048], "bfloat16"), "mc": ("sbuf", [128, 2048], "bfloat16"), "ks": ("sbuf", [128, 2048], "bfloat16"),
    "a00": ("sbuf", [128, 1024], "bfloat16"), "a01": ("sbuf", [128, 1024], "bfloat16"),
    "a10": ("sbuf", [128, 1024], "float32"), "a11": ("sbuf", [128, 1024], "float32"),
    "U0": ("sbuf", [128, SMAX], "bfloat16"), "Z0": ("sbuf", [128, SMAX], "bfloat16"),
    "U1": ("sbuf", [128, SMAX], "float32"), "Z1": ("sbuf", [128, SMAX], "float32"),
    "YS": ("sbuf", [128, 1024], "float32"),
    "rs6": ("sbuf", [128, 384], "float32"), "rs7": ("sbuf", [128, 7 * 512], "bfloat16"),
    "one": ("sbuf", [128, 160], "bfloat16"), "D": ("sbuf", [128, 160], "bfloat16"),
    "S1": ("sbuf", [128, 160], "bfloat16"), "S2": ("sbuf", [128, 160], "bfloat16"), "St": ("sbuf", [128, 160], "bfloat16"),
    "Dt": ("sbuf", [128, 160], "bfloat16"),
    "MT": ("sbuf", [128, 8 * 128], "bfloat16"), "MF": ("sbuf", [128, 2 * 128], "float32"),
    "pint": ("sbuf", [128, 8], "int32"), "tcol": ("sbuf", [128, 8], "float32"), "n16": ("sbuf", [128, 16], "int32"),
    "jc": ("sbuf", [128, 24], "int32"), "jf": ("sbuf", [128, 24], "float32"), "jg": ("sbuf", [128, 24], "float32"),
    "ji": ("sbuf", [128, 24], "int32"), "bc": ("sbuf", [128, 24], "uint16"),
    "Req": ("sbuf", [128, 16], "float32"), "Rlt": ("sbuf", [128, 16], "float32"), "Rge": ("sbuf", [128, 16], "float32"),
    "X0": ("psum", [128, 512], "float32"), "X1": ("psum", [128, 512], "float32"), "X2": ("psum", [128, 512], "float32"),
    "P0": ("psum", [128, 512], "float32"), "P1": ("psum", [128, 512], "float32"),
    "Q0": ("psum", [128, 512], "float32"), "Q1": ("psum", [128, 512], "float32"),
}
SEMAPHORES = ["sv", "sa", "sp", "sg", "gd", "l1", "l2", "l3", "r1", "r2", "r3"] + ["d%d" % i for i in range(20)]


def order(nodes):
    return sorted(nodes, key=lambda n: ORDER.index(n["key"]))


def rank_program(g, core, T, topo):
    r = T.rank_of(core)
    if r is None:
        return
    v, a, pe, sy = g.vector, g.scalar, g.tensor, g.sync
    Q = {"v": v, "a": a, "p": pe, "s": sy, "g": g}
    nodes, ndma = [], [0]

    def node(name, q, deps, fn, sem=None, inc=1, key=None):
        n = {"name": name, "key": key or name, "q": q, "deps": [d for d in deps if d is not None], "fn": fn, "sem": sem or "s" + q, "inc": inc}
        nodes.append(n)
        return n

    def V(name, deps, fn):
        return node(name, "v", deps, fn)

    def copy(name, q, out, in_, deps, key=None):
        if q == "v":
            return node(name, q, deps, lambda: v.tensor_copy(out, in_), key=key)
        return node(name, q, deps, lambda: a.activation(out, in_, Act.Copy), key=key)

    def dma(name, q, pairs, deps):
        s = "d%d" % ndma[0]
        ndma[0] += 1

        def fn():
            for o, i in pairs:
                Q[q].dma_start(o, i).then_inc(T.sem[s], 16)
        return node(name, q, deps, fn, sem=s, inc=16 * len(pairs))

    def mm(name, calls, deps):
        def fn():
            ins = None
            for c in calls:
                ins = pe.matmul(*c)
            return ins
        return node(name, "p", deps, fn)

    def exchange(k, src, dst, w, deps):
        trs, used = [], [0, 0]
        for q in range(N):
            if q == r:
                continue
            c = T.cores[q]
            e = topo.engines(core, c)
            near = 0 if topo.die(c) != topo.die(core) else 1
            b = 4 * used[near] + near
            used[near] += 1
            rid, pid, _ = topo.addr(c)
            trs.append(RemoteDMATransfer(dst_ids=[DstId(rid=rid, pnc=pid)], dma_engine_mask=(1 << e[b]) | (1 << e[b + 2]),
                                         remote_sem=T.sem["r%d" % k], src=src[:, q * w:(q + 1) * w], dst=dst))

        def fn():
            g.remote_dma_fused(trs, local_sem=T.sem["l%d" % k])
        node("send%d" % k, "g", deps, fn, sem="l%d" % k, inc=14)
        return node("arr%d" % k, "x%d" % k, deps, None, sem="r%d" % k, inc=14)

    def handover(name, stage, win, offs, w, deps):
        cw = w // 16
        cols = [c for c in range(N * cw) if c // cw != r]
        h = len(cols) // 2
        res = []
        for q, part in (("v", cols[:h]), ("a", cols[h:])):
            runs = []
            for c in part:
                if runs and runs[-1][1] == c:
                    runs[-1][1] = c + 1
                else:
                    runs.append([c, c + 1])
            for c0, c1 in runs:
                res.append(copy("%s%s%d" % (name, q, c0), q, stage[:, 16 * c0:16 * c1], win.indirect(offs[:, c0:c1]), deps, key=name + q))
        return res

    l_sup = dma("l_sup", "s", [(T.W1[:, 0:M], T.sup[:, :])], [])
    l_ship = dma("l_ship", "a", [(T.ship32[:, :], T.ship[:, :])], [])

    def loads(l, deps):
        lp = dma("l_p%d" % l, "s", [(T.p32[:, l], T.parts[:, 768 * l:768 * (l + 1)])], deps)
        pr = []
        for h in range(2):
            b, ld = l * A + h * 512, h + 1
            pr += [(T.cs[0:128 - ld, b:b + 512], T.cap[ld:128, b:b + 512]), (T.cs[128 - ld:128, b:b + 512], T.cap[0:ld, b:b + 512])]
        lc = dma("l_c%d" % l, "s", pr, deps)
        lk = dma("l_k%d" % l, "s", [(T.ks[:, l * A:(l + 1) * A], T.stock[:, l * A:(l + 1) * A])], deps)
        return lp, lc, lk
    ld = [loads(0, [])]

    i_p = node("i_p", "g", [], lambda: g.iota(T.pint[:, 0:1], [[0, 1]], 0, 1))
    i_n = node("i_n", "g", [], lambda: g.iota(T.n16[:, :], [[1, 16]], 0, 0))
    i_j = node("i_j", "g", [], lambda: g.iota(T.jc[:, :], [[16, 24]], 0, 0))
    one = V("one", [], lambda: v.memset(T.one[:, :], 1.0))
    d1 = node("d1", "g", [one], lambda: g.affine_select(T.Dt[:, :], T.one[:, :], [[1, 160]], Op.is_equal, 0.0, -16, -1))
    dg = node("d2", "g", [d1], lambda: g.affine_select(T.D[:, :], T.Dt[:, :], [[1, 160]], Op.not_equal, 1.0, 112, -1))
    t1 = V("t1", [i_p], lambda: v.tensor_scalar(T.pint[:, 4:5], T.pint[:, 0:1], 15, None, Op.bitwise_and))
    tc = V("tc", [t1], lambda: v.tensor_copy(T.tcol[:, 0:1], T.pint[:, 4:5]))
    tcol = T.tcol[:, 0:1]
    req = V("req", [tc, i_n], lambda: v.tensor_scalar(T.Req[:, :], T.n16[:, :], tcol, None, Op.is_equal))
    rlt = V("rlt", [tc, i_n], lambda: v.tensor_scalar(T.Rlt[:, :], T.n16[:, :], tcol, None, Op.is_gt))
    rge = V("rge", [tc, i_n], lambda: v.tensor_scalar(T.Rge[:, :], T.n16[:, :], tcol, None, Op.is_le))
    j1 = V("j1", [tc, i_j], lambda: v.tensor_scalar(T.jf[:, :], T.jc[:, :], tcol, -2.5, Op.add, Op.add))
    j2 = V("j2", [j1], lambda: v.tensor_scalar(T.jg[:, :], T.jf[:, :], 1.0 / 6.0, None, Op.mult))
    j3 = V("j3", [j2], lambda: v.tensor_copy(T.ji[:, :], T.jg[:, :]))
    bc = V("bc", [j3], lambda: v.tensor_copy(T.bc[:, :], T.ji[:, :]))
    view = lambda s: T.D[:, 16 - s:144 - s]
    col = lambda t, n: t[:, n:n + 1]

    def masked(name, out, src, m, dep):
        return V(name, [dg, dep], lambda: v.tensor_scalar(out, src, m, None, Op.mult))
    mt = lambda i: T.MT[:, 128 * i:128 * (i + 1)]
    mf = lambda i: T.MF[:, 128 * i:128 * (i + 1)]
    s1 = masked("S1", T.S1[:, :], T.D[:, :], col(T.Req, 15), req)
    st = masked("St", T.St[:, 16:160], T.D[:, 15:159], col(T.Req, 14), req)
    s2 = V("S2", [s1, st], lambda: v.tensor_tensor(T.S2[:, 16:160], T.S1[:, 16:160], T.St[:, 16:160], Op.add))
    neg = masked("neg", mt(0), view(0), -1.0, None)
    bm = masked("B", mt(1), view(-1), col(T.Req, 15), req)
    sh = [masked("Sh%d" % h, mt(2 + h), view(h + 1), col(T.Rlt, 15 - h), rlt) for h in range(2)]
    mk = [masked("Mk%d" % h, mt(4 + h), view(h + 1), col(T.Rge, 15 - h), rge) for h in range(2)]
    am = [masked("A%d" % h, mt(6 + h), view(h + 1), col(T.Req, 14 - h), req) for h in range(2)]
    sf = [masked("Sf%d" % h, mf(h), view(h + 1), col(T.Rlt, 15 - h), rlt) for h in range(2)]
    z6 = V("z6", [], lambda: v.memset(T.rs6[:, :], 0.0))
    r6 = V("r6", [z6], lambda: v.memset(T.rs6[:, 0:384:6], BIG))
    smax = 7 * max([32] + [c[1] - c[0] for p in PC for c in p if c[2] == "S"])
    z7 = V("z7", [], lambda: v.memset(T.rs7[:, 0:smax], 0.0))
    r7 = V("r7", [z7], lambda: v.memset(T.rs7[:, 0:smax:7], BIG))

    su = V("su", [l_ship], lambda: v.tensor_copy(T.shipu[:, :], T.ship32[:, :]))
    raw = T.W1[:, 0:M]
    gs = handover("gs", T.SH, raw, T.shipu, SR, [su, l_sup])
    arr1 = exchange(1, T.SH, T.W1[:, M + r * SR:M + (r + 1) * SR], SR, gs)
    own1 = copy("own1", "a", T.W1[:, M + r * SR:M + (r + 1) * SR], raw.indirect(T.shipu[:, 16 * r:16 * (r + 1)]), gs)
    wp1 = node("wp1", "a", [req] + gs, lambda: a.activation(T.WP[:, 0:M], raw, Act.Identity, scale=col(T.Req, 15)))
    z8 = V("z8", gs, lambda: v.memset(T.WP[:, M:2 * M], 0.0))
    wp2 = dma("wp2", "s", [(T.WP[15:128:16, M:2 * M], T.W1[15:128:16, M:2 * M])], [arr1, own1, z8])
    l_hand = dma("l_hand", "s", [(T.hand32[:, :], T.hand[:, :])], [arr1])
    ld.append(loads(1, [arr1]))
    cast = node("cast", "g", [arr1, own1, l_hand], lambda: g.dma_start(T.W2[:, 0:2 * M], T.W1[:, 0:2 * M]), sem="gd", inc=16)

    state = {"x": [None] * 3, "nx": 0, "p": [None] * 4, "q": [None] * 2}

    def level(l, win1, win2, ready1, ready2, late, sel, dsel):
        lp, lc, lk = ld[l]
        Vb = T["V%d" % l]
        o1 = [copy("o1_%d_%d" % (l, i), "v", T.off1[:, 384 * l + i:384 * (l + 1):6], T.p32[:, l, i, :], [lp] + late) for i in range(C)]
        dl = V("dl%d" % l, [lp] + late, lambda: v.tensor_tensor(T.delta[:, l], T.p32[:, l, 6:12], T.p32[:, l, 0:6], Op.subtract))
        mcn = V("mc%d" % l, [lc] + late, lambda: v.tensor_scalar(T.mc[:, l * A:(l + 1) * A], T.cs[:, l * A:(l + 1) * A], 0.0, None, Op.min))
        lists = []
        for k, (a0, a1, share) in enumerate(CH[l]):
            nm = "%d_%d" % (l, k)
            c0, c1 = a0 // 16, a1 // 16
            nc, b = c1 - c0, 384 * l + 6 * c0
            w = 6 * nc
            cut = w - share
            g1 = [copy("g1a" + nm, "a", Vb[:, 96 * c0:96 * c0 + 16 * cut], win1.indirect(T.off1[:, b:b + cut]), o1 + ready1)]
            for x in range(cut, w, PIECE):
                y = min(w, x + PIECE)
                g1.append(copy("g1v%s_%d" % (nm, x), "v", Vb[:, 96 * c0 + 16 * x:96 * c0 + 16 * y], win1.indirect(T.off1[:, b + x:b + y]), o1 + ready1))
            xb = state["nx"] % 3
            state["nx"] += 1
            X = T["X%d" % xb]
            ext = mm("ext" + nm, [(X[:, 0:w], sel[:, 31 - p:159 - p], Vb[:, 96 * c0 + p:96 * c1:16], p == 0, p == 15) for p in range(16)],
                     g1 + [dsel, state["x"][xb]])
            Mn, eq, m5 = T.Mn[:, b:b + w], T.eq[:, b:b + w], T.M5[:, 64 * l + c0:64 * l + c1]
            scn = V("scn" + nm, [ext, r6], lambda X=X, w=w, Mn=Mn: v.tensor_tensor_scan(Mn, T.rs6[:, 0:w], X[:, 0:w], 0.0, Op.add, Op.min))
            low = copy("low" + nm, "v", m5, T.Mn[:, b + 5:b + w:6], [scn])
            eqn = V("eq" + nm, [low, bc], lambda w=w, Mn=Mn, eq=eq, m5=m5: v.tensor_tensor(eq, m5.indirect(T.bc[:, 0:w // 16]), Mn, Op.is_equal))
            calls = []
            for i in range(C):
                o = X[:, i * nc:(i + 1) * nc]
                calls.append((o, view(0), T.eq[:, b + i:b + w:6], True, i == 0))
                if i:
                    calls.append((o, mt(0), T.eq[:, b + i - 1:b + w:6], False, True))
            hit = mm("hit" + nm, calls, [eqn, neg])
            mul = V("mul" + nm, [hit, dl], lambda X=X, w=w, c0=c0, c1=c1: v.tensor_tensor(X[:, 0:w], X[:, 0:w], T.delta[:, l, :, c0:c1], Op.mult))
            add = V("add" + nm, [mul], lambda X=X, w=w, c0=c0, c1=c1: v.tensor_tensor(X[:, 0:w], X[:, 0:w], T.p32[:, l, 0:6, c0:c1], Op.add))
            cnv = copy("cnv" + nm, "v", T.off2[:, b:b + w], X[:, 0:w], [add])
            state["x"][xb] = cnv
            lists.append((c0, c1, b, cnv))
        results, u0 = [], 0
        for k, (a0, a1, way) in enumerate(PC[l]):
            nm, n = "%d_%d" % (l, k), a1 - a0
            c0, c1, b, cnv = [x for x in lists if x[0] <= a0 // 16 < x[1]][0]
            lst = [T.off2[:, b + i * (c1 - c0) + a0 // 16 - c0:b + i * (c1 - c0) + a1 // 16 - c0] for i in range(C)]
            cap = T.cs[:, l * A + a0:l * A + a1]
            if way == "F":
                prev, res = lc, cap
                for i in range(C):
                    o = T["a%d%d" % (l, i % 2)][:, a0:a1]
                    prev = V("g2%s_%d" % (nm, i), [prev, cnv] + ready2, lambda o=o, off=lst[i], src=res: v.tensor_tensor(o, win2.indirect(off), src, Op.min))
                    res = o
            else:
                U, Z, u1 = T["U%d" % l], T["Z%d" % l], u0 + 7 * n
                cp = copy("cp" + nm, "a", U[:, u0:u1:7], cap, [lc] + late)
                g2 = [copy("g2%s_%d" % (nm, i), "a", U[:, u0 + 1 + i:u1:7], win2.indirect(lst[i]), [cnv, cp] + ready2) for i in range(C)]
                prev = V("red" + nm, g2 + [r7],
                         lambda n=n, U=U[:, u0:u1], Z=Z[:, u0:u1]: v.tensor_tensor_scan(Z, T.rs7[:, 0:7 * n], U, 0.0, Op.add, Op.min))
                res = Z[:, u0 + 6:u1:7]
                u0 = u1
            h = a0 // 512
            kk, mc = T.ks[:, l * A + a0:l * A + a1], T.mc[:, l * A + a0:l * A + a1]
            if l == 0:
                P, Qb = T["P%d" % h][:, a0 - 512 * h:a1 - 512 * h], T["Q%d" % (k % 2)][:, 0:n]
                preq = mm("prq" + nm, [(Qb, mt(1), kk, True, False)], [lk, bm, state["q"][k % 2], cnv])
                finq = mm("fnq" + nm, [(Qb, mt(6 + h), res, False, True)], [preq, prev, am[h]])
                fin = mm("fin" + nm, [(P, view(0), kk, True, False), (P, mt(4 + h), mc, False, False), (P, mt(2 + h), res, False, True)],
                         [lk, mcn, mk[h], prev, sh[h], finq])
                evq = copy("evq" + nm, "v" if k == len(PC[l]) - 1 else "a", T.WP[:, 2 * M + a0:2 * M + a1], Qb, [finq])
                state["q"][k % 2] = evq
                results.append((evq, finq, fin))
            else:
                P = T[("P0", "P1", "Q0", "Q1")[k % 4]][:, 0:n]
                pre = mm("pre" + nm, [(P, view(0), kk, True, False), (P, mt(4 + h), mc, False, False)], [lk, mcn, mk[h], state["p"][k % 4], cnv])
                fin = mm("fin" + nm, [(P, mf(h), res, False, True)], [pre, prev, sf[h]])
                ev = copy("ev" + nm, "a", T.YS[:, a0:a1], P, [fin])
                dma("st" + nm, "s", [(T.y[:, a0:a1], T.YS[:, a0:a1])], [ev])
                state["p"][k % 4] = ev
        return results

    res = level(0, T.W1[:, :], T.W1[:, :], [arr1, own1], [], gs, T.S1, s1)
    hu = copy("hu", "v", T.handu[:, :], T.hand32[:, :], [l_hand, res[1][1]])
    b1, sl = 2 * M, 2 * M + A + r * SA
    ha = handover("ha", T.HA, T.WP[:, b1:b1 + A], T.handu, SA, [hu] + [x[0] for x in res])
    arr2 = exchange(2, T.HA, T.WP[:, sl:sl + SA], SA, ha)
    evp = [copy("evp%d" % h, "va"[h], T.W2[:, b1 + 512 * h:b1 + 512 * (h + 1)], T["P%d" % h][:, :], ha + [x[2] for x in res]) for h in range(2)]
    state["p"] = evp + state["q"]
    hb = handover("hb", T.HB, T.W2[:, b1:b1 + A], T.handu, SA, evp)
    arr3 = exchange(3, T.HB, T.W2[:, sl:sl + SA], SA, hb)
    own2 = copy("own2", "a", T.WP[:, sl:sl + SA], T.WP[:, b1:b1 + A].indirect(T.handu[:, 8 * r:8 * (r + 1)]), hb)
    own3 = copy("own3", "a", T.W2[:, sl:sl + SA], T.W2[:, b1:b1 + A].indirect(T.handu[:, 8 * r:8 * (r + 1)]), hb)
    level(1, T.WP[:, :], T.W2[:, :], [arr2, own2, wp1, wp2], [arr3, own3, cast], hb, T.S2, s2)

    count, waited, token = {}, {}, {}
    for n in order(nodes):
        if n["fn"] is not None:
            need = {}
            for d in n["deps"]:
                s, c = token[d["name"]]
                need[s] = max(need.get(s, 0), c)
            for s, c in need.items():
                if waited.get((n["q"], s), 0) < c:
                    Q[n["q"]].wait_ge(T.sem[s], c)
                    waited[(n["q"], s)] = c
            ins = n["fn"]()
            if ins is not None:
                ins.then_inc(T.sem[n["sem"]], n["inc"])
        count[n["sem"]] = count.get(n["sem"], 0) + n["inc"]
        token[n["name"]] = (n["sem"], count[n["sem"]])
    for s, c in count.items():
        if max([w for (q, x), w in waited.items() if x == s] + [0]) < c:
            sy.wait_ge(T.sem[s], c)
